import numpy as np
import ml_dtypes


def mxq(x, axis, fmt="e4m3"):
    dtype, down = {"e4m3": (ml_dtypes.float8_e4m3fn, 7), "e5m2": (ml_dtypes.float8_e5m2, 14)}[fmt]
    v = np.moveaxis(np.asarray(x, np.float32).astype(ml_dtypes.bfloat16).astype(np.float64), axis, -1)
    blocks = v.reshape(v.shape[:-1] + (-1, 32))
    amax = np.abs(blocks).max(-1, keepdims=True)
    byte = np.maximum(np.where(amax > 0, np.frexp(amax)[1] - 1 + 127, 0) - down, 1)
    scale = np.exp2(byte - 127.0)
    codes = (blocks / scale).astype(np.float32).astype(dtype).astype(np.float64)
    return np.moveaxis((codes * scale).reshape(v.shape), -1, axis)


WIDE = False


def mx_kscale(k):
    if not WIDE:
        return np.ones(k)
    levels = np.array([10, -10, 5, -5, 0])
    if k % 512:
        return np.exp2(np.random.permutation(np.resize(levels, k // 32))).repeat(32)
    a = np.empty((k // 512, 16))
    for p in range(k // 512):
        a[p, :8] = np.random.permutation(np.resize(levels, 8))
        for g in range(8):
            far = levels[np.abs(levels - a[p, g]) >= 10]
            a[p, g + 8] = far[np.random.randint(len(far))]
    return np.exp2(a.ravel()).repeat(32)


def f64(x):
    return np.asarray(x).astype(np.float64)


def striped(idx):
    return np.tile(idx.reshape(-1, 16).T, (8, 1)).astype(np.uint16)


def unstriped(offs):
    return offs[:16].T.reshape(-1).astype(np.int64)


def striped8(idx):
    return np.concatenate([x.reshape(-1, 16).T for x in idx]).astype(np.uint16)


def runs(offs, k):
    lists = np.stack([offs[16 * r : 16 * r + 16].T.reshape(-1) for r in range(8)]).astype(np.int64)
    return lists[np.arange(k) % 512 // 64]


def pack_weight(w):
    k, n = w.shape
    w = f64(np.asarray(w, np.float32).astype(ml_dtypes.bfloat16)).reshape(k // 32, 32, n)
    amax = np.abs(w).max(1)
    byte = np.clip(np.where(amax > 0, np.frexp(amax)[1] - 1 + 127 - 7, 1), 1, 254)
    scaled = (w * np.exp2(127.0 - byte)[:, None, :]).reshape(k, n).astype(np.float32)
    words = np.ascontiguousarray(scaled.reshape(k // 512, 128, 4, n).transpose(0, 1, 3, 2)).astype(ml_dtypes.float8_e4m3fn).view(np.uint8)
    return words, np.ascontiguousarray(byte.astype(np.uint8).reshape(k // 512, 16, n))


def unpack_weight(words, scales):
    g, p, n, _ = words.shape
    vals = np.ascontiguousarray(words).view(ml_dtypes.float8_e4m3fn).astype(np.float64) * np.repeat(np.exp2(scales.astype(np.float64) - 127.0), 8, axis=1)[..., None]
    return vals.transpose(0, 1, 3, 2).reshape(g * 512, n)


K, T, S, G, H, C = 512, 1024, 512, 2048, 512, 512


def setup_inputs():
    n = np.random.standard_normal
    s = mx_kscale(K)[:, None]
    packed_xT = pack_weight(n((K, T)) * s)
    packed_dT = pack_weight(n((K, G)) / s)
    return {
        "x_words": packed_xT[0],
        "x_scales": packed_xT[1],
        "d_words": packed_dT[0],
        "d_scales": packed_dT[1],
        "gs": (np.random.uniform(0.5, 1.5, (K, 1)) / s).astype(np.float32),
        "offs": striped(np.random.permutation(T)[:S]),
        "k1": striped8(np.random.randint(0, G, (8, H))),
        "n1": striped8(np.stack([np.random.permutation(S) for _ in range(8)])),
        "n2": striped8(np.stack([np.random.permutation(S) for _ in range(8)])),
        "n3": striped8(np.stack([np.random.permutation(S) for _ in range(8)])),
        "cand": striped(np.random.permutation(T)[:C]),
        "n4": striped8(np.stack([np.random.permutation(S) for _ in range(8)])),
        "n5": striped8(np.stack([np.random.permutation(S) for _ in range(8)])),
    }


def reference(x_words, x_scales, d_words, d_scales, gs, offs, k1, n1, n2, n3, cand, n4, n5):
    x_cand = unpack_weight(x_words, x_scales)[:, unstriped(cand)]
    d_k1 = unpack_weight(d_words, d_scales)[np.arange(K)[:, None], runs(k1, K)]
    xq = unpack_weight(x_words, x_scales)[:, unstriped(offs)]
    h = 0.0625 * (d_k1.T @ xq)
    z = f64(gs) * (0.75 * (h * (h[np.arange(H)[:, None], runs(n1, H)]) + (h[np.arange(H)[:, None], runs(n2, H)]) * (h[np.arange(H)[:, None], runs(n3, H)])))
    s = 0.0625 * ((x_cand.T @ mxq(z, 0, "e4m3")))
    return np.maximum(s[np.arange(C)[:, None], runs(n4, C)], s[np.arange(C)[:, None], runs(n5, C)]) - (0.75 * s)

@@ -1,0 +1,182 @@
+from contextlib import ExitStack
+
+import concourse.mybir as mybir
+
+K, T, S, G, H, C = 512, 1024, 512, 2048, 512, 512
+FLOPS = 2 * K * H * S + 2 * H * C * S
+
+F32 = mybir.dt.float32
+BF16 = mybir.dt.bfloat16
+I32 = mybir.dt.int32
+U32 = mybir.dt.uint32
+U16 = mybir.dt.uint16
+U8 = mybir.dt.uint8
+FP8X4 = mybir.dt.float8_e4m3fn_x4
+MULT = mybir.AluOpType.mult
+ADD = mybir.AluOpType.add
+MAX = mybir.AluOpType.max
+COPY = mybir.ActivationFunctionType.Copy
+
+P = 128
+PACK = 4
+HALF = S // 2
+LIST_COLS = S // 16
+
+
+def tile_picked_pqcdotover_none_p_kernel(
+    tc, x_words, x_scales, d_words, d_scales, gs, offs, k1, n1, n2, n3, cand, n4, n5, out
+):
+    nc = tc.nc
+    with ExitStack() as ctx:
+        lists = ctx.enter_context(tc.tile_pool(name="lists", bufs=1))
+        keep = ctx.enter_context(tc.tile_pool(name="keep", bufs=1))
+        psum = ctx.enter_context(tc.psum_pool(name="psum", bufs=1))
+
+        def load_list(name, source):
+            tile = lists.tile([P, LIST_COLS], U16, name=name)
+            nc.sync.dma_start(tile[:], source)
+            return tile
+
+        def half_of(tile, part):
+            return tile[:, part * LIST_COLS // 2 : (part + 1) * LIST_COLS // 2]
+
+        d_scale_table = keep.tile([P, G], U8, align_bytes=64)
+        x_scale_table = keep.tile([P, T], U8, align_bytes=64)
+        d_scale_plane = keep.tile([P, H], U8, align_bytes=64)
+        nc.gpsimd.memset(d_scale_table[:].bitcast(I32), 0)
+        nc.vector.memset(x_scale_table[:].bitcast(I32), 0)
+        nc.gpsimd.memset(d_scale_plane[:].bitcast(I32), 0)
+
+        k1_list = load_list("k1_list", k1)
+        nc.sync.dma_start(d_scale_table[0:P:8, :].bitcast(I32), d_scales[0].bitcast(I32))
+        offs_list = load_list("offs_list", offs)
+        x_scale_rows = x_scales[0].bitcast(I32).rearrange("(q b) c -> b q c", b=PACK)
+        for b in range(PACK):
+            nc.sync.dma_start(x_scale_table[b:P:32, :].bitcast(I32), x_scale_rows[b])
+        d_word_table = keep.tile([P, G], I32, align_bytes=64)
+        x_word_table = keep.tile([P, T], I32, align_bytes=64)
+        nc.sync.dma_start(d_word_table[:], d_words[0].rearrange("p c r -> p (c r)").bitcast(I32))
+        nc.sync.dma_start(x_word_table[:], x_words[0].rearrange("p c r -> p (c r)").bitcast(I32))
+        cand_list = load_list("cand_list", cand)
+        gain = keep.tile([P, PACK], F32)
+        nc.sync.dma_start(gain[:], gs.rearrange("(p t) o -> p (t o)", t=PACK))
+        n2_list = load_list("n2_list", n2)
+        n1_list = load_list("n1_list", n1)
+        n3_list = load_list("n3_list", n3)
+        n4_list = load_list("n4_list", n4)
+        n5_list = load_list("n5_list", n5)
+
+        gain_scaled = keep.tile([P, PACK], F32)
+        nc.scalar.activation(gain_scaled[:], gain[:], COPY, scale=0.75 * 0.0625)
+
+        d_scale_picked = keep.tile([P, H], U8, align_bytes=64)
+        nc.vector.tensor_copy(d_scale_picked[:], d_scale_table[:].indirect(k1_list[:]))
+        d_scale_dealt = keep.tile([P, H], U8, align_bytes=64)
+        nc.vector.tensor_copy(
+            d_scale_dealt[:].rearrange("p (t m) -> p m t", t=PACK),
+            d_scale_picked[:].rearrange("p (m t) -> p m t", t=PACK),
+        )
+        for b in range(PACK):
+            nc.scalar.dma_start(d_scale_plane[b:P:32, :].bitcast(I32), d_scale_dealt[8 * b : P : 32, :].bitcast(I32))
+
+        xq_scales = keep.tile([P, S], U8, align_bytes=64)
+        nc.vector.tensor_copy(xq_scales[:], x_scale_table[:].indirect(offs_list[:]))
+        d_picked = keep.tile([P, H], U32, align_bytes=64, tag="picked_words")
+        nc.vector.tensor_copy(d_picked[:], d_word_table[:].bitcast(U32).indirect(k1_list[:]))
+        xq_words = keep.tile([P, S], U32, align_bytes=64)
+        nc.vector.tensor_copy(xq_words[:], x_word_table[:].bitcast(U32).indirect(offs_list[:]))
+        d_dealt = keep.tile([P, H], U32, align_bytes=64)
+        nc.vector.tensor_copy(
+            d_dealt[:].rearrange("p (t m) -> p m t", t=PACK),
+            d_picked[:].rearrange("p (m t) -> p m t", t=PACK),
+        )
+
+        h_tiles, hg_tiles = [], []
+        for t in range(PACK):
+            bank = psum.tile([P, S], F32, name=f"h_bank{t}")
+            cols = slice(t * P, (t + 1) * P)
+            nc.tensor.matmul_mx(
+                bank[:],
+                lhsT=d_dealt[:, cols].bitcast(FP8X4),
+                lhsT_scale=d_scale_plane[:, cols],
+                rhs=xq_words[:].bitcast(FP8X4),
+                rhs_scale=xq_scales[:],
+                start=True,
+                stop=True,
+            )
+            h = keep.tile([P, S], F32, name=f"h{t}")
+            hg = keep.tile([P, S], F32, name=f"hg{t}")
+            nc.scalar.activation(h[:], bank[:], COPY, scale=0.0625)
+            nc.scalar.activation(hg[:], bank[:], COPY, scale=gain_scaled[:, t : t + 1])
+            h_tiles.append(h)
+            hg_tiles.append(hg)
+
+        cand_words = keep.tile([P, C], U32, align_bytes=64, tag="picked_words")
+        nc.vector.tensor_copy(
+            cand_words[:].rearrange("p (t a b) -> p a t b", t=PACK, b=PACK),
+            x_word_table[:].bitcast(U32).indirect(cand_list[:]),
+        )
+        cand_scale_picked = keep.tile([P, C], U8, align_bytes=64)
+        nc.vector.tensor_copy(cand_scale_picked[:], x_scale_table[:].indirect(cand_list[:]))
+        cand_scales = keep.tile([P, C], U8, align_bytes=64)
+        nc.vector.tensor_copy(
+            cand_scales[:].bitcast(I32).rearrange("p (t a) -> p a t", t=PACK),
+            cand_scale_picked[:].bitcast(I32).rearrange("p (a t) -> p a t", t=PACK),
+        )
+
+        s_banks = [psum.tile([P, S], F32, name=f"s_bank{t}") for t in range(PACK)]
+        s_tiles = [keep.tile([P, S], F32, name=f"s{t}") for t in range(PACK)]
+        sneg_tiles = [keep.tile([P, S], F32, name=f"sneg{t}") for t in range(PACK)]
+        for part in range(2):
+            cols = slice(part * HALF, (part + 1) * HALF)
+            first = keep.tile([P, PACK, HALF], F32, name=f"first{part}")
+            second = keep.tile([P, PACK, HALF], F32, name=f"second{part}")
+            for t in range(PACK):
+                fetched = keep.tile([P, HALF], F32, name=f"fetched{part}_{t}")
+                nc.vector.tensor_copy(fetched[:], h_tiles[t][:].indirect(half_of(n2_list, part)))
+                nc.vector.tensor_tensor(first[:, t, :], h_tiles[t][:].indirect(half_of(n1_list, part)), hg_tiles[t][:, cols], MULT)
+                nc.vector.tensor_tensor(second[:, t, :], hg_tiles[t][:].indirect(half_of(n3_list, part)), fetched[:], MULT)
+            z = keep.tile([P, HALF, PACK], BF16, name=f"z{part}", align_bytes=64)
+            nc.vector.tensor_tensor(
+                z[:].rearrange("p (c i) t -> p c t i", i=2),
+                first[:].rearrange("p t (c i) -> p c t i", i=2),
+                second[:].rearrange("p t (c i) -> p c t i", i=2),
+                ADD,
+            )
+            z_words = keep.tile([P, HALF], U32, name=f"z_words{part}", align_bytes=64)
+            z_scales = keep.tile([P, HALF], U8, name=f"z_scales{part}", align_bytes=64)
+            nc.vector.quantize_mx(z_words[:].bitcast(FP8X4), z_scales[:], z[:].rearrange("p j t -> p (j t)"))
+            for t in range(PACK):
+                rows = slice(t * P, (t + 1) * P)
+                nc.tensor.matmul_mx(
+                    s_banks[t][:, cols],
+                    lhsT=cand_words[:, rows].bitcast(FP8X4),
+                    lhsT_scale=cand_scales[:, rows],
+                    rhs=z_words[:].bitcast(FP8X4),
+                    rhs_scale=z_scales[:],
+                    start=True,
+                    stop=True,
+                )
+                nc.scalar.activation(s_tiles[t][:, cols], s_banks[t][:, cols], COPY, scale=0.0625)
+                nc.scalar.activation(sneg_tiles[t][:, cols], s_banks[t][:, cols], COPY, scale=-0.75 * 0.0625)
+
+        out_rows = out.rearrange("(a t b) j -> t a b j", t=PACK, b=PACK)
+        pending = []
+
+        def finish():
+            t, cols, left, right = pending.pop(0)
+            result = keep.tile([P, HALF], F32, name=f"result{t}_{cols.start}")
+            nc.vector.tensor_tensor(result[:], left[:], right[:], MAX)
+            nc.sync.dma_start(out_rows[t][:, :, cols], result[:])
+
+        for t in range(PACK):
+            for part in range(2):
+                cols = slice(part * HALF, (part + 1) * HALF)
+                left = keep.tile([P, HALF], F32, name=f"left{t}_{part}")
+                right = keep.tile([P, HALF], F32, name=f"right{t}_{part}")
+                nc.vector.tensor_tensor(left[:], s_tiles[t][:].indirect(half_of(n4_list, part)), sneg_tiles[t][:, cols], ADD)
+                if pending:
+                    finish()
+                nc.vector.tensor_tensor(right[:], s_tiles[t][:].indirect(half_of(n5_list, part)), sneg_tiles[t][:, cols], ADD)
+                pending.append((t, cols, left, right))
+        finish()

@@ -1,6 +1,7 @@
 from contextlib import ExitStack
 
 import concourse.mybir as mybir
+from concourse.masks import make_identity
 
 K, T, S, G, H, C = 512, 1024, 512, 2048, 512, 512
 FLOPS = 2 * K * H * S + 2 * H * C * S
@@ -15,11 +16,14 @@ FP8X4 = mybir.dt.float8_e4m3fn_x4
 MULT = mybir.AluOpType.mult
 ADD = mybir.AluOpType.add
 MAX = mybir.AluOpType.max
+SUBTRACT = mybir.AluOpType.subtract
+RELU = mybir.ActivationFunctionType.Relu
 COPY = mybir.ActivationFunctionType.Copy
 
 P = 128
 PACK = 4
 HALF = S // 2
+EARLY = 3 * P
 LIST_COLS = S // 16
 
 
@@ -30,6 +34,7 @@ def tile_picked_pqcdotover_none_p_kernel(
     with ExitStack() as ctx:
         lists = ctx.enter_context(tc.tile_pool(name="lists", bufs=1))
         keep = ctx.enter_context(tc.tile_pool(name="keep", bufs=1))
+        shared = ctx.enter_context(tc.tile_pool(name="shared", bufs=1))
         psum = ctx.enter_context(tc.psum_pool(name="psum", bufs=1))
 
         def load_list(name, source):
@@ -40,12 +45,23 @@ def tile_picked_pqcdotover_none_p_kernel(
         def half_of(tile, part):
             return tile[:, part * LIST_COLS // 2 : (part + 1) * LIST_COLS // 2]
 
+        def add_transposed(target, terms):
+            for n, term in enumerate(terms):
+                nc.tensor.matmul(target, term, identity[:], start=n == 0, stop=n == len(terms) - 1, is_transpose=True)
+
         d_scale_table = keep.tile([P, G], U8, align_bytes=64)
         x_scale_table = keep.tile([P, T], U8, align_bytes=64)
         d_scale_plane = keep.tile([P, H], U8, align_bytes=64)
         nc.gpsimd.memset(d_scale_table[:].bitcast(I32), 0)
-        nc.vector.memset(x_scale_table[:].bitcast(I32), 0)
+        nc.gpsimd.memset(x_scale_table[:].bitcast(I32), 0)
+        gain = keep.tile([P, PACK], F32)
+        nc.gpsimd.dma_start(gain[:], gs.rearrange("(p t) o -> p (t o)", t=PACK))
         nc.gpsimd.memset(d_scale_plane[:].bitcast(I32), 0)
+        identity = keep.tile([P, P], F32)
+        make_identity(nc, identity[:])
+        s_tiles = [keep.tile([P, S if t < 2 else 2 * S], F32, name=f"s{t}") for t in range(PACK)]
+        for window in s_tiles[2:]:
+            nc.vector.memset(window[:, S:], 0.0)
 
         k1_list = load_list("k1_list", k1)
         nc.sync.dma_start(d_scale_table[0:P:8, :].bitcast(I32), d_scales[0].bitcast(I32))
@@ -58,8 +74,6 @@ def tile_picked_pqcdotover_none_p_kernel(
         nc.sync.dma_start(d_word_table[:], d_words[0].rearrange("p c r -> p (c r)").bitcast(I32))
         nc.sync.dma_start(x_word_table[:], x_words[0].rearrange("p c r -> p (c r)").bitcast(I32))
         cand_list = load_list("cand_list", cand)
-        gain = keep.tile([P, PACK], F32)
-        nc.sync.dma_start(gain[:], gs.rearrange("(p t) o -> p (t o)", t=PACK))
         n2_list = load_list("n2_list", n2)
         n1_list = load_list("n1_list", n1)
         n3_list = load_list("n3_list", n3)
@@ -73,27 +87,27 @@ def tile_picked_pqcdotover_none_p_kernel(
         nc.vector.tensor_copy(d_scale_picked[:], d_scale_table[:].indirect(k1_list[:]))
         d_scale_dealt = keep.tile([P, H], U8, align_bytes=64)
         nc.vector.tensor_copy(
-            d_scale_dealt[:].rearrange("p (t m) -> p m t", t=PACK),
-            d_scale_picked[:].rearrange("p (m t) -> p m t", t=PACK),
+            d_scale_dealt[:].rearrange("p (t m) -> p t m", t=PACK),
+            d_scale_picked[:].rearrange("p (m t) -> p t m", t=PACK),
         )
         for b in range(PACK):
             nc.scalar.dma_start(d_scale_plane[b:P:32, :].bitcast(I32), d_scale_dealt[8 * b : P : 32, :].bitcast(I32))
 
         xq_scales = keep.tile([P, S], U8, align_bytes=64)
         nc.vector.tensor_copy(xq_scales[:], x_scale_table[:].indirect(offs_list[:]))
-        d_picked = keep.tile([P, H], U32, align_bytes=64, tag="picked_words")
+        d_picked = shared.tile([P, H], U32, align_bytes=64, offset=0)
         nc.vector.tensor_copy(d_picked[:], d_word_table[:].bitcast(U32).indirect(k1_list[:]))
         xq_words = keep.tile([P, S], U32, align_bytes=64)
         nc.vector.tensor_copy(xq_words[:], x_word_table[:].bitcast(U32).indirect(offs_list[:]))
         d_dealt = keep.tile([P, H], U32, align_bytes=64)
         nc.vector.tensor_copy(
-            d_dealt[:].rearrange("p (t m) -> p m t", t=PACK),
-            d_picked[:].rearrange("p (m t) -> p m t", t=PACK),
+            d_dealt[:].rearrange("p (t a i) -> p a t i", t=PACK, i=PACK),
+            d_picked[:].rearrange("p (a i t) -> p a t i", t=PACK, i=PACK),
         )
 
         h_tiles, hg_tiles = [], []
         for t in range(PACK):
-            bank = psum.tile([P, S], F32, name=f"h_bank{t}")
+            bank = psum.tile([P, S], F32, name=f"h_bank{t}", tag=f"bank{t}")
             cols = slice(t * P, (t + 1) * P)
             nc.tensor.matmul_mx(
                 bank[:],
@@ -111,12 +125,12 @@ def tile_picked_pqcdotover_none_p_kernel(
             h_tiles.append(h)
             hg_tiles.append(hg)
 
-        cand_words = keep.tile([P, C], U32, align_bytes=64, tag="picked_words")
+        cand_words = shared.tile([P, C], U32, align_bytes=64, offset=C)
         nc.vector.tensor_copy(
             cand_words[:].rearrange("p (t a b) -> p a t b", t=PACK, b=PACK),
             x_word_table[:].bitcast(U32).indirect(cand_list[:]),
         )
-        cand_scale_picked = keep.tile([P, C], U8, align_bytes=64)
+        cand_scale_picked = shared.tile([P, C], U8, align_bytes=64, offset=0)
         nc.vector.tensor_copy(cand_scale_picked[:], x_scale_table[:].indirect(cand_list[:]))
         cand_scales = keep.tile([P, C], U8, align_bytes=64)
         nc.vector.tensor_copy(
@@ -124,59 +138,124 @@ def tile_picked_pqcdotover_none_p_kernel(
             cand_scale_picked[:].bitcast(I32).rearrange("p (a t) -> p a t", t=PACK),
         )
 
-        s_banks = [psum.tile([P, S], F32, name=f"s_bank{t}") for t in range(PACK)]
-        s_tiles = [keep.tile([P, S], F32, name=f"s{t}") for t in range(PACK)]
-        sneg_tiles = [keep.tile([P, S], F32, name=f"sneg{t}") for t in range(PACK)]
-        for part in range(2):
-            cols = slice(part * HALF, (part + 1) * HALF)
-            first = keep.tile([P, PACK, HALF], F32, name=f"first{part}")
-            second = keep.tile([P, PACK, HALF], F32, name=f"second{part}")
-            for t in range(PACK):
-                fetched = keep.tile([P, HALF], F32, name=f"fetched{part}_{t}")
-                nc.vector.tensor_copy(fetched[:], h_tiles[t][:].indirect(half_of(n2_list, part)))
-                nc.vector.tensor_tensor(first[:, t, :], h_tiles[t][:].indirect(half_of(n1_list, part)), hg_tiles[t][:, cols], MULT)
-                nc.vector.tensor_tensor(second[:, t, :], hg_tiles[t][:].indirect(half_of(n3_list, part)), fetched[:], MULT)
-            z = keep.tile([P, HALF, PACK], BF16, name=f"z{part}", align_bytes=64)
-            nc.vector.tensor_tensor(
-                z[:].rearrange("p (c i) t -> p c t i", i=2),
-                first[:].rearrange("p t (c i) -> p c t i", i=2),
-                second[:].rearrange("p t (c i) -> p c t i", i=2),
-                ADD,
+        z_words = keep.tile([P, S], U32, align_bytes=64)
+        z_scales = keep.tile([P, S], U8, align_bytes=64)
+
+        def score(t, cols):
+            rows = slice(t * P, (t + 1) * P)
+            nc.tensor.matmul_mx(
+                s_banks[t][:, cols],
+                lhsT=cand_words[:, rows].bitcast(FP8X4),
+                lhsT_scale=cand_scales[:, rows],
+                rhs=z_words[:, cols].bitcast(FP8X4),
+                rhs_scale=z_scales[:, cols],
+                start=True,
+                stop=True,
             )
-            z_words = keep.tile([P, HALF], U32, name=f"z_words{part}", align_bytes=64)
-            z_scales = keep.tile([P, HALF], U8, name=f"z_scales{part}", align_bytes=64)
-            nc.vector.quantize_mx(z_words[:].bitcast(FP8X4), z_scales[:], z[:].rearrange("p j t -> p (j t)"))
+
+        sneg_tiles = [keep.tile([P, S], F32, name=f"sneg{t}") for t in range(PACK)]
+        def products(cols):
+            width = cols.stop - cols.start
+            entries = slice(cols.start // 16, cols.stop // 16)
+            first = keep.tile([P, PACK, width], F32, name=f"first{cols.start}")
+            second = keep.tile([P, PACK, width], F32, name=f"second{cols.start}")
             for t in range(PACK):
-                rows = slice(t * P, (t + 1) * P)
-                nc.tensor.matmul_mx(
-                    s_banks[t][:, cols],
-                    lhsT=cand_words[:, rows].bitcast(FP8X4),
-                    lhsT_scale=cand_scales[:, rows],
-                    rhs=z_words[:].bitcast(FP8X4),
-                    rhs_scale=z_scales[:],
-                    start=True,
-                    stop=True,
-                )
-                nc.scalar.activation(s_tiles[t][:, cols], s_banks[t][:, cols], COPY, scale=0.0625)
-                nc.scalar.activation(sneg_tiles[t][:, cols], s_banks[t][:, cols], COPY, scale=-0.75 * 0.0625)
+                fetched = keep.tile([P, width], F32, name=f"fetched{cols.start}_{t}")
+                nc.vector.tensor_copy(fetched[:], h_tiles[t][:].indirect(n2_list[:, entries]))
+                nc.vector.tensor_tensor(first[:, t, :], h_tiles[t][:].indirect(n1_list[:, entries]), hg_tiles[t][:, cols], MULT)
+                nc.vector.tensor_tensor(second[:, t, :], hg_tiles[t][:].indirect(n3_list[:, entries]), fetched[:], MULT)
+            return first, second
+
+        def quantise(z, cols, start):
+            inside = slice(cols.start - start, cols.stop - start)
+            nc.vector.quantize_mx(z_words[:, cols].bitcast(FP8X4), z_scales[:, cols], z[:, inside, :].rearrange("p j t -> p (j t)"))
+
+        first, second = products(slice(0, EARLY))
+        z_early = keep.tile([P, EARLY, PACK], BF16, tag="z", align_bytes=64)
+        blocks = [slice(n * P, (n + 1) * P) for n in range(EARLY // P)]
+        sum_banks = [psum.tile([P, 2, 2, P], F32, name=f"sum_bank{n}", tag=f"bank{n}") for n in range(len(blocks))]
+        word_banks = [psum.tile([P, 2, P], F32, name=f"word_bank{n}", tag=f"bank{len(blocks) + n}") for n in range(len(blocks))]
+        for u in range(2):
+            for e in range(2):
+                for n, block in enumerate(blocks):
+                    add_transposed(sum_banks[n][:, u, e, :], [first[:, 2 * u + e, block], second[:, 2 * u + e, block]])
+            for n, block in enumerate(blocks):
+                pairs = keep.tile([P, P, 2], BF16, name=f"pairs{u}_{n}")
+                nc.scalar.copy(pairs[:], sum_banks[n][:, u].rearrange("j e p -> j p e"))
+                nc.tensor.transpose(word_banks[n][:, u, :], pairs[:].rearrange("j p e -> j (p e)").bitcast(F32), identity[:])
+                if u == 1:
+                    nc.scalar.copy(
+                        z_early[:, block, :].rearrange("p j t -> p (j t)").bitcast(F32).rearrange("p (j u) -> p j u", u=2),
+                        word_banks[n][:].rearrange("p u j -> p j u"),
+                    )
+        s_banks = [psum.tile([P, S], F32, name=f"s_bank{t}", tag=f"bank{PACK + t}") for t in range(PACK)]
+        for cols in (slice(0, HALF), slice(HALF, EARLY)):
+            quantise(z_early, cols, 0)
+            score(0, cols)
+        nc.scalar.activation(s_tiles[0][:, :EARLY], s_banks[0][:, :EARLY], COPY, scale=0.0625)
+
+        late = slice(EARLY, S)
+        first, second = products(late)
+        z_late = keep.tile([P, S - EARLY, PACK], BF16, tag="z", align_bytes=64)
+        nc.vector.tensor_tensor(
+            z_late[:].rearrange("p (c i) t -> p c t i", i=2),
+            first[:].rearrange("p t (c i) -> p c t i", i=2),
+            second[:].rearrange("p t (c i) -> p c t i", i=2),
+            ADD,
+        )
+        quantise(z_late, late, EARLY)
+        score(0, late)
+        nc.scalar.activation(s_tiles[0][:, late], s_banks[0][:, late], COPY, scale=0.0625)
+        nc.scalar.activation(sneg_tiles[0][:], s_banks[0][:], COPY, scale=-0.75 * 0.0625)
+        for t in range(1, PACK):
+            score(t, slice(0, HALF))
+            score(t, slice(HALF, S))
+            nc.scalar.activation(s_tiles[t][:, :S], s_banks[t][:], COPY, scale=0.0625)
+            nc.scalar.activation(sneg_tiles[t][:], s_banks[t][:], COPY, scale=-0.75 * 0.0625)
 
         out_rows = out.rearrange("(a t b) j -> t a b j", t=PACK, b=PACK)
-        pending = []
-
-        def finish():
-            t, cols, left, right = pending.pop(0)
-            result = keep.tile([P, HALF], F32, name=f"result{t}_{cols.start}")
-            nc.vector.tensor_tensor(result[:], left[:], right[:], MAX)
-            nc.sync.dma_start(out_rows[t][:, :, cols], result[:])
-
-        for t in range(PACK):
+        for t in range(2):
+            larger_of = []
+            for part in range(2):
+                left = keep.tile([P, HALF], F32, name=f"plain{t}_{part}")
+                nc.vector.tensor_copy(left[:], s_tiles[t][:].indirect(half_of(n4_list, part)))
+                larger_of.append(left)
             for part in range(2):
                 cols = slice(part * HALF, (part + 1) * HALF)
-                left = keep.tile([P, HALF], F32, name=f"left{t}_{part}")
-                right = keep.tile([P, HALF], F32, name=f"right{t}_{part}")
-                nc.vector.tensor_tensor(left[:], s_tiles[t][:].indirect(half_of(n4_list, part)), sneg_tiles[t][:, cols], ADD)
-                if pending:
-                    finish()
-                nc.vector.tensor_tensor(right[:], s_tiles[t][:].indirect(half_of(n5_list, part)), sneg_tiles[t][:, cols], ADD)
-                pending.append((t, cols, left, right))
-        finish()
+                excess = keep.tile([P, HALF], F32, name=f"excess{t}_{part}")
+                nc.vector.tensor_tensor(excess[:], s_tiles[t][:].indirect(half_of(n5_list, part)), larger_of[part][:], SUBTRACT)
+                positive = keep.tile([P, HALF], F32, name=f"positive{t}_{part}")
+                nc.scalar.activation(positive[:], excess[:], RELU)
+                turned_bank = psum.tile([P, HALF], F32, name=f"turned_bank{t}_{part}", tag=f"bank{2 * t + part}")
+                for block in range(2):
+                    piece = slice(block * P, (block + 1) * P)
+                    add_transposed(turned_bank[:, piece], [larger_of[part][:, piece], sneg_tiles[t][:, cols][:, piece], positive[:, piece]])
+                turned = keep.tile([P, HALF], F32, name=f"turned{t}_{part}")
+                nc.scalar.copy(turned[:], turned_bank[:])
+                result_bank = psum.tile([P, HALF], F32, name=f"result_bank{t}_{part}", tag=f"bank{PACK + 2 * t + part}")
+                for block in range(2):
+                    piece = slice(block * P, (block + 1) * P)
+                    nc.tensor.transpose(result_bank[:, piece], turned[:, piece], identity[:])
+                result = keep.tile([P, HALF], F32, name=f"result{t}_{part}")
+                nc.scalar.copy(result[:], result_bank[:])
+                nc.scalar.dma_start(out_rows[t][:, :, cols], result[:])
+
+        def with_own_term(t, entries, cols, name):
+            tile = keep.tile([P, cols.stop - cols.start], F32, name=name)
+            nc.vector.tensor_tensor(tile[:], s_tiles[t][:].indirect(entries), sneg_tiles[t][:, cols], ADD)
+            return tile
+
+        def store_larger(t, cols, left, right):
+            result = keep.tile([P, cols.stop - cols.start], F32, name=f"larger{t}_{cols.start}")
+            nc.vector.tensor_tensor(result[:], left, right, MAX)
+            nc.sync.dma_start(out_rows[t][:, :, cols], result[:])
+
+        whole = slice(0, S)
+        halves = [slice(0, HALF), slice(HALF, S)]
+        left2 = with_own_term(2, n4_list[:], whole, "left2")
+        right2 = with_own_term(2, n5_list[:], whole, "right2")
+        left3 = with_own_term(3, n4_list[:], whole, "left3")
+        store_larger(2, whole, left2[:], right2[:])
+        right3 = [with_own_term(3, half_of(n5_list, part), halves[part], f"right3_{part}") for part in range(2)]
+        for part in range(2):
+            store_larger(3, halves[part], left3[:, halves[part]], right3[part][:])

@@ -141,10 +141,14 @@ def tile_picked_pqcdotover_none_p_kernel(
         z_words = keep.tile([P, S], U32, align_bytes=64)
         z_scales = keep.tile([P, S], U8, align_bytes=64)
 
-        def score(t, cols):
+        def empty_scores(t, cols, bank):
+            nc.scalar.activation(s_tiles[t][:, cols], bank, COPY, scale=0.0625)
+            nc.scalar.activation(sneg_tiles[t][:, cols], bank, COPY, scale=-0.75 * 0.0625)
+
+        def score(t, cols, bank):
             rows = slice(t * P, (t + 1) * P)
             nc.tensor.matmul_mx(
-                s_banks[t][:, cols],
+                bank,
                 lhsT=cand_words[:, rows].bitcast(FP8X4),
                 lhsT_scale=cand_scales[:, rows],
                 rhs=z_words[:, cols].bitcast(FP8X4),
@@ -191,8 +195,8 @@ def tile_picked_pqcdotover_none_p_kernel(
         s_banks = [psum.tile([P, S], F32, name=f"s_bank{t}", tag=f"bank{PACK + t}") for t in range(PACK)]
         for cols in (slice(0, HALF), slice(HALF, EARLY)):
             quantise(z_early, cols, 0)
-            score(0, cols)
-        nc.scalar.activation(s_tiles[0][:, :EARLY], s_banks[0][:, :EARLY], COPY, scale=0.0625)
+            score(0, cols, s_banks[0][:, cols])
+        empty_scores(0, slice(0, EARLY), s_banks[0][:, :EARLY])
 
         late = slice(EARLY, S)
         first, second = products(late)
@@ -204,41 +208,41 @@ def tile_picked_pqcdotover_none_p_kernel(
             ADD,
         )
         quantise(z_late, late, EARLY)
-        score(0, late)
-        nc.scalar.activation(s_tiles[0][:, late], s_banks[0][:, late], COPY, scale=0.0625)
-        nc.scalar.activation(sneg_tiles[0][:], s_banks[0][:], COPY, scale=-0.75 * 0.0625)
-        for t in range(1, PACK):
-            score(t, slice(0, HALF))
-            score(t, slice(HALF, S))
-            nc.scalar.activation(s_tiles[t][:, :S], s_banks[t][:], COPY, scale=0.0625)
-            nc.scalar.activation(sneg_tiles[t][:], s_banks[t][:], COPY, scale=-0.75 * 0.0625)
+        late_bank = psum.tile([P, S - EARLY], F32, tag="bank0")
+        score(0, late, late_bank[:])
+        empty_scores(0, late, late_bank[:])
+
+        whole = slice(0, S)
+        halves = [slice(0, HALF), slice(HALF, S)]
+
+        def score_whole(t):
+            score(t, whole, s_banks[t][:])
+            empty_scores(t, whole, s_banks[t][:])
 
         out_rows = out.rearrange("(a t b) j -> t a b j", t=PACK, b=PACK)
-        for t in range(2):
-            larger_of = []
-            for part in range(2):
-                left = keep.tile([P, HALF], F32, name=f"plain{t}_{part}")
-                nc.vector.tensor_copy(left[:], s_tiles[t][:].indirect(half_of(n4_list, part)))
-                larger_of.append(left)
-            for part in range(2):
-                cols = slice(part * HALF, (part + 1) * HALF)
-                excess = keep.tile([P, HALF], F32, name=f"excess{t}_{part}")
-                nc.vector.tensor_tensor(excess[:], s_tiles[t][:].indirect(half_of(n5_list, part)), larger_of[part][:], SUBTRACT)
-                positive = keep.tile([P, HALF], F32, name=f"positive{t}_{part}")
-                nc.scalar.activation(positive[:], excess[:], RELU)
-                turned_bank = psum.tile([P, HALF], F32, name=f"turned_bank{t}_{part}", tag=f"bank{2 * t + part}")
-                for block in range(2):
-                    piece = slice(block * P, (block + 1) * P)
-                    add_transposed(turned_bank[:, piece], [larger_of[part][:, piece], sneg_tiles[t][:, cols][:, piece], positive[:, piece]])
-                turned = keep.tile([P, HALF], F32, name=f"turned{t}_{part}")
-                nc.scalar.copy(turned[:], turned_bank[:])
-                result_bank = psum.tile([P, HALF], F32, name=f"result_bank{t}_{part}", tag=f"bank{PACK + 2 * t + part}")
-                for block in range(2):
-                    piece = slice(block * P, (block + 1) * P)
-                    nc.tensor.transpose(result_bank[:, piece], turned[:, piece], identity[:])
-                result = keep.tile([P, HALF], F32, name=f"result{t}_{part}")
-                nc.scalar.copy(result[:], result_bank[:])
-                nc.scalar.dma_start(out_rows[t][:, :, cols], result[:])
+
+        def fetch_plain(t, part):
+            plain = keep.tile([P, HALF], F32, name=f"plain{t}_{part}")
+            nc.vector.tensor_copy(plain[:], s_tiles[t][:].indirect(half_of(n4_list, part)))
+            return plain
+
+        def finish_on_tensor(t, part, plain, banks):
+            cols = halves[part]
+            excess = keep.tile([P, HALF], F32, name=f"excess{t}_{part}")
+            nc.vector.tensor_tensor(excess[:], s_tiles[t][:].indirect(half_of(n5_list, part)), plain[:], SUBTRACT)
+            positive = keep.tile([P, HALF], F32, name=f"positive{t}_{part}")
+            nc.scalar.activation(positive[:], excess[:], RELU)
+            turned_bank = psum.tile([P, HALF], F32, name=f"turned_bank{t}_{part}", tag=f"bank{banks[0]}")
+            for block in blocks[:2]:
+                add_transposed(turned_bank[:, block], [plain[:, block], sneg_tiles[t][:, cols][:, block], positive[:, block]])
+            turned = keep.tile([P, HALF], F32, name=f"turned{t}_{part}")
+            nc.scalar.copy(turned[:], turned_bank[:])
+            result_bank = psum.tile([P, HALF], F32, name=f"result_bank{t}_{part}", tag=f"bank{banks[1]}")
+            for block in blocks[:2]:
+                nc.tensor.transpose(result_bank[:, block], turned[:, block], identity[:])
+            result = keep.tile([P, HALF], F32, name=f"result{t}_{part}")
+            nc.scalar.copy(result[:], result_bank[:])
+            nc.scalar.dma_start(out_rows[t][:, :, cols], result[:])
 
         def with_own_term(t, entries, cols, name):
             tile = keep.tile([P, cols.stop - cols.start], F32, name=name)
@@ -250,12 +254,17 @@ def tile_picked_pqcdotover_none_p_kernel(
             nc.vector.tensor_tensor(result[:], left, right, MAX)
             nc.sync.dma_start(out_rows[t][:, :, cols], result[:])
 
-        whole = slice(0, S)
-        halves = [slice(0, HALF), slice(HALF, S)]
-        left2 = with_own_term(2, n4_list[:], whole, "left2")
-        right2 = with_own_term(2, n5_list[:], whole, "right2")
-        left3 = with_own_term(3, n4_list[:], whole, "left3")
-        store_larger(2, whole, left2[:], right2[:])
-        right3 = [with_own_term(3, half_of(n5_list, part), halves[part], f"right3_{part}") for part in range(2)]
-        for part in range(2):
-            store_larger(3, halves[part], left3[:, halves[part]], right3[part][:])
+        score_whole(1)
+        score_whole(2)
+        plain0 = [fetch_plain(0, part) for part in range(2)]
+        finish_on_tensor(0, 0, plain0[0], (1, 4))
+        finish_on_tensor(0, 1, plain0[1], (2, 0))
+        score_whole(3)
+        plain1 = [fetch_plain(1, part) for part in range(2)]
+        finish_on_tensor(1, 0, plain1[0], (3, 5))
+        finish_on_tensor(1, 1, plain1[1], (6, 1))
+        for t in range(2, PACK):
+            left = with_own_term(t, n4_list[:], whole, f"left{t}")
+            right = [with_own_term(t, half_of(n5_list, part), halves[part], f"right{t}_{part}") for part in range(2)]
+            for part in range(2):
+                store_larger(t, halves[part], left[:, halves[part]], right[part][:])

from contextlib import ExitStack

import concourse.mybir as mybir
from concourse.masks import make_identity

K, T, S, G, H, C = 512, 1024, 512, 2048, 512, 512
FLOPS = 2 * K * H * S + 2 * H * C * S

F32 = mybir.dt.float32
BF16 = mybir.dt.bfloat16
I32 = mybir.dt.int32
U32 = mybir.dt.uint32
U16 = mybir.dt.uint16
U8 = mybir.dt.uint8
FP8X4 = mybir.dt.float8_e4m3fn_x4
MULT = mybir.AluOpType.mult
ADD = mybir.AluOpType.add
MAX = mybir.AluOpType.max
SUBTRACT = mybir.AluOpType.subtract
RELU = mybir.ActivationFunctionType.Relu
COPY = mybir.ActivationFunctionType.Copy

P = 128
PACK = 4
HALF = S // 2
EARLY = 3 * P
LIST_COLS = S // 16


def tile_picked_pqcdotover_none_p_kernel(
    tc, x_words, x_scales, d_words, d_scales, gs, offs, k1, n1, n2, n3, cand, n4, n5, out
):
    nc = tc.nc
    with ExitStack() as ctx:
        lists = ctx.enter_context(tc.tile_pool(name="lists", bufs=1))
        keep = ctx.enter_context(tc.tile_pool(name="keep", bufs=1))
        shared = ctx.enter_context(tc.tile_pool(name="shared", bufs=1))
        psum = ctx.enter_context(tc.psum_pool(name="psum", bufs=1))

        def load_list(name, source):
            tile = lists.tile([P, LIST_COLS], U16, name=name)
            nc.sync.dma_start(tile[:], source)
            return tile

        def half_of(tile, part):
            return tile[:, part * LIST_COLS // 2 : (part + 1) * LIST_COLS // 2]

        def add_transposed(target, terms):
            for n, term in enumerate(terms):
                nc.tensor.matmul(target, term, identity[:], start=n == 0, stop=n == len(terms) - 1, is_transpose=True)

        d_scale_table = keep.tile([P, G], U8, align_bytes=64)
        x_scale_table = keep.tile([P, T], U8, align_bytes=64)
        d_scale_plane = keep.tile([P, H], U8, align_bytes=64)
        nc.gpsimd.memset(d_scale_table[:].bitcast(I32), 0)
        nc.gpsimd.memset(x_scale_table[:].bitcast(I32), 0)
        gain = keep.tile([P, PACK], F32)
        nc.gpsimd.dma_start(gain[:], gs.rearrange("(p t) o -> p (t o)", t=PACK))
        nc.gpsimd.memset(d_scale_plane[:].bitcast(I32), 0)
        identity = keep.tile([P, P], F32)
        make_identity(nc, identity[:])
        s_tiles = [keep.tile([P, S if t < 2 else 2 * S], F32, name=f"s{t}") for t in range(PACK)]
        for window in s_tiles[2:]:
            nc.vector.memset(window[:, S:], 0.0)

        k1_list = load_list("k1_list", k1)
        nc.sync.dma_start(d_scale_table[0:P:8, :].bitcast(I32), d_scales[0].bitcast(I32))
        offs_list = load_list("offs_list", offs)
        x_scale_rows = x_scales[0].bitcast(I32).rearrange("(q b) c -> b q c", b=PACK)
        for b in range(PACK):
            nc.sync.dma_start(x_scale_table[b:P:32, :].bitcast(I32), x_scale_rows[b])
        d_word_table = keep.tile([P, G], I32, align_bytes=64)
        x_word_table = keep.tile([P, T], I32, align_bytes=64)
        nc.sync.dma_start(d_word_table[:], d_words[0].rearrange("p c r -> p (c r)").bitcast(I32))
        nc.sync.dma_start(x_word_table[:], x_words[0].rearrange("p c r -> p (c r)").bitcast(I32))
        cand_list = load_list("cand_list", cand)
        n2_list = load_list("n2_list", n2)
        n1_list = load_list("n1_list", n1)
        n3_list = load_list("n3_list", n3)
        n4_list = load_list("n4_list", n4)
        n5_list = load_list("n5_list", n5)

        gain_scaled = keep.tile([P, PACK], F32)
        nc.scalar.activation(gain_scaled[:], gain[:], COPY, scale=0.75 * 0.0625)

        d_scale_picked = keep.tile([P, H], U8, align_bytes=64)
        nc.vector.tensor_copy(d_scale_picked[:], d_scale_table[:].indirect(k1_list[:]))
        d_scale_dealt = keep.tile([P, H], U8, align_bytes=64)
        nc.vector.tensor_copy(
            d_scale_dealt[:].rearrange("p (t m) -> p t m", t=PACK),
            d_scale_picked[:].rearrange("p (m t) -> p t m", t=PACK),
        )
        for b in range(PACK):
            nc.scalar.dma_start(d_scale_plane[b:P:32, :].bitcast(I32), d_scale_dealt[8 * b : P : 32, :].bitcast(I32))

        xq_scales = keep.tile([P, S], U8, align_bytes=64)
        nc.vector.tensor_copy(xq_scales[:], x_scale_table[:].indirect(offs_list[:]))
        d_picked = shared.tile([P, H], U32, align_bytes=64, offset=0)
        nc.vector.tensor_copy(d_picked[:], d_word_table[:].bitcast(U32).indirect(k1_list[:]))
        xq_words = keep.tile([P, S], U32, align_bytes=64)
        nc.vector.tensor_copy(xq_words[:], x_word_table[:].bitcast(U32).indirect(offs_list[:]))
        d_dealt = keep.tile([P, H], U32, align_bytes=64)
        nc.vector.tensor_copy(
            d_dealt[:].rearrange("p (t a i) -> p a t i", t=PACK, i=PACK),
            d_picked[:].rearrange("p (a i t) -> p a t i", t=PACK, i=PACK),
        )

        h_tiles, hg_tiles = [], []
        for t in range(PACK):
            bank = psum.tile([P, S], F32, name=f"h_bank{t}", tag=f"bank{t}")
            cols = slice(t * P, (t + 1) * P)
            nc.tensor.matmul_mx(
                bank[:],
                lhsT=d_dealt[:, cols].bitcast(FP8X4),
                lhsT_scale=d_scale_plane[:, cols],
                rhs=xq_words[:].bitcast(FP8X4),
                rhs_scale=xq_scales[:],
                start=True,
                stop=True,
            )
            h = keep.tile([P, S], F32, name=f"h{t}")
            hg = keep.tile([P, S], F32, name=f"hg{t}")
            nc.scalar.activation(h[:], bank[:], COPY, scale=0.0625)
            nc.scalar.activation(hg[:], bank[:], COPY, scale=gain_scaled[:, t : t + 1])
            h_tiles.append(h)
            hg_tiles.append(hg)

        cand_words = shared.tile([P, C], U32, align_bytes=64, offset=C)
        nc.vector.tensor_copy(
            cand_words[:].rearrange("p (t a b) -> p a t b", t=PACK, b=PACK),
            x_word_table[:].bitcast(U32).indirect(cand_list[:]),
        )
        cand_scale_picked = shared.tile([P, C], U8, align_bytes=64, offset=0)
        nc.vector.tensor_copy(cand_scale_picked[:], x_scale_table[:].indirect(cand_list[:]))
        cand_scales = keep.tile([P, C], U8, align_bytes=64)
        nc.vector.tensor_copy(
            cand_scales[:].bitcast(I32).rearrange("p (t a) -> p a t", t=PACK),
            cand_scale_picked[:].bitcast(I32).rearrange("p (a t) -> p a t", t=PACK),
        )

        z_words = keep.tile([P, S], U32, align_bytes=64)
        z_scales = keep.tile([P, S], U8, align_bytes=64)

        def empty_scores(t, cols, bank):
            nc.scalar.activation(s_tiles[t][:, cols], bank, COPY, scale=0.0625)
            nc.scalar.activation(sneg_tiles[t][:, cols], bank, COPY, scale=-0.75 * 0.0625)

        def score(t, cols, bank):
            rows = slice(t * P, (t + 1) * P)
            nc.tensor.matmul_mx(
                bank,
                lhsT=cand_words[:, rows].bitcast(FP8X4),
                lhsT_scale=cand_scales[:, rows],
                rhs=z_words[:, cols].bitcast(FP8X4),
                rhs_scale=z_scales[:, cols],
                start=True,
                stop=True,
            )

        sneg_tiles = [keep.tile([P, S], F32, name=f"sneg{t}") for t in range(PACK)]
        def products(cols):
            width = cols.stop - cols.start
            entries = slice(cols.start // 16, cols.stop // 16)
            first = keep.tile([P, PACK, width], F32, name=f"first{cols.start}")
            second = keep.tile([P, PACK, width], F32, name=f"second{cols.start}")
            for t in range(PACK):
                fetched = keep.tile([P, width], F32, name=f"fetched{cols.start}_{t}")
                nc.vector.tensor_copy(fetched[:], h_tiles[t][:].indirect(n2_list[:, entries]))
                nc.vector.tensor_tensor(first[:, t, :], h_tiles[t][:].indirect(n1_list[:, entries]), hg_tiles[t][:, cols], MULT)
                nc.vector.tensor_tensor(second[:, t, :], hg_tiles[t][:].indirect(n3_list[:, entries]), fetched[:], MULT)
            return first, second

        def quantise(z, cols, start):
            inside = slice(cols.start - start, cols.stop - start)
            nc.vector.quantize_mx(z_words[:, cols].bitcast(FP8X4), z_scales[:, cols], z[:, inside, :].rearrange("p j t -> p (j t)"))

        first, second = products(slice(0, EARLY))
        z_early = keep.tile([P, EARLY, PACK], BF16, tag="z", align_bytes=64)
        blocks = [slice(n * P, (n + 1) * P) for n in range(EARLY // P)]
        sum_banks = [psum.tile([P, 2, 2, P], F32, name=f"sum_bank{n}", tag=f"bank{n}") for n in range(len(blocks))]
        word_banks = [psum.tile([P, 2, P], F32, name=f"word_bank{n}", tag=f"bank{len(blocks) + n}") for n in range(len(blocks))]
        for u in range(2):
            for e in range(2):
                for n, block in enumerate(blocks):
                    add_transposed(sum_banks[n][:, u, e, :], [first[:, 2 * u + e, block], second[:, 2 * u + e, block]])
            for n, block in enumerate(blocks):
                pairs = keep.tile([P, P, 2], BF16, name=f"pairs{u}_{n}")
                nc.scalar.copy(pairs[:], sum_banks[n][:, u].rearrange("j e p -> j p e"))
                nc.tensor.transpose(word_banks[n][:, u, :], pairs[:].rearrange("j p e -> j (p e)").bitcast(F32), identity[:])
                if u == 1:
                    nc.scalar.copy(
                        z_early[:, block, :].rearrange("p j t -> p (j t)").bitcast(F32).rearrange("p (j u) -> p j u", u=2),
                        word_banks[n][:].rearrange("p u j -> p j u"),
                    )
        s_banks = [psum.tile([P, S], F32, name=f"s_bank{t}", tag=f"bank{PACK + t}") for t in range(PACK)]
        for cols in (slice(0, HALF), slice(HALF, EARLY)):
            quantise(z_early, cols, 0)
            score(0, cols, s_banks[0][:, cols])
        empty_scores(0, slice(0, EARLY), s_banks[0][:, :EARLY])

        late = slice(EARLY, S)
        first, second = products(late)
        z_late = keep.tile([P, S - EARLY, PACK], BF16, tag="z", align_bytes=64)
        nc.vector.tensor_tensor(
            z_late[:].rearrange("p (c i) t -> p c t i", i=2),
            first[:].rearrange("p t (c i) -> p c t i", i=2),
            second[:].rearrange("p t (c i) -> p c t i", i=2),
            ADD,
        )
        quantise(z_late, late, EARLY)
        late_bank = psum.tile([P, S - EARLY], F32, tag="bank0")
        score(0, late, late_bank[:])
        empty_scores(0, late, late_bank[:])

        whole = slice(0, S)
        halves = [slice(0, HALF), slice(HALF, S)]

        def score_whole(t):
            score(t, whole, s_banks[t][:])
            empty_scores(t, whole, s_banks[t][:])

        out_rows = out.rearrange("(a t b) j -> t a b j", t=PACK, b=PACK)

        def fetch_plain(t, part):
            plain = keep.tile([P, HALF], F32, name=f"plain{t}_{part}")
            nc.vector.tensor_copy(plain[:], s_tiles[t][:].indirect(half_of(n4_list, part)))
            return plain

        def finish_on_tensor(t, part, plain, banks):
            cols = halves[part]
            excess = keep.tile([P, HALF], F32, name=f"excess{t}_{part}")
            nc.vector.tensor_tensor(excess[:], s_tiles[t][:].indirect(half_of(n5_list, part)), plain[:], SUBTRACT)
            positive = keep.tile([P, HALF], F32, name=f"positive{t}_{part}")
            nc.scalar.activation(positive[:], excess[:], RELU)
            turned_bank = psum.tile([P, HALF], F32, name=f"turned_bank{t}_{part}", tag=f"bank{banks[0]}")
            for block in blocks[:2]:
                add_transposed(turned_bank[:, block], [plain[:, block], sneg_tiles[t][:, cols][:, block], positive[:, block]])
            turned = keep.tile([P, HALF], F32, name=f"turned{t}_{part}")
            nc.scalar.copy(turned[:], turned_bank[:])
            result_bank = psum.tile([P, HALF], F32, name=f"result_bank{t}_{part}", tag=f"bank{banks[1]}")
            for block in blocks[:2]:
                nc.tensor.transpose(result_bank[:, block], turned[:, block], identity[:])
            result = keep.tile([P, HALF], F32, name=f"result{t}_{part}")
            nc.scalar.copy(result[:], result_bank[:])
            nc.scalar.dma_start(out_rows[t][:, :, cols], result[:])

        def with_own_term(t, entries, cols, name):
            tile = keep.tile([P, cols.stop - cols.start], F32, name=name)
            nc.vector.tensor_tensor(tile[:], s_tiles[t][:].indirect(entries), sneg_tiles[t][:, cols], ADD)
            return tile

        def store_larger(t, cols, left, right):
            result = keep.tile([P, cols.stop - cols.start], F32, name=f"larger{t}_{cols.start}")
            nc.vector.tensor_tensor(result[:], left, right, MAX)
            nc.sync.dma_start(out_rows[t][:, :, cols], result[:])

        score_whole(1)
        score_whole(2)
        plain0 = [fetch_plain(0, part) for part in range(2)]
        finish_on_tensor(0, 0, plain0[0], (1, 4))
        finish_on_tensor(0, 1, plain0[1], (2, 0))
        score_whole(3)
        plain1 = [fetch_plain(1, part) for part in range(2)]
        finish_on_tensor(1, 0, plain1[0], (3, 5))
        finish_on_tensor(1, 1, plain1[1], (6, 1))
        for t in range(2, PACK):
            left = with_own_term(t, n4_list[:], whole, f"left{t}")
            right = [with_own_term(t, half_of(n5_list, part), halves[part], f"right{t}_{part}") for part in range(2)]
            for part in range(2):
                store_larger(t, halves[part], left[:, halves[part]], right[part][:])
